import numpy as np
import ml_dtypes


def mxq(x, axis, fmt="e4m3"):
    dtype, down = {"e4m3": (ml_dtypes.float8_e4m3fn, 7), "e5m2": (ml_dtypes.float8_e5m2, 14)}[fmt]
    v = np.moveaxis(np.asarray(x, np.float32).astype(ml_dtypes.bfloat16).astype(np.float64), axis, -1)
    blocks = v.reshape(v.shape[:-1] + (-1, 32))
    amax = np.abs(blocks).max(-1, keepdims=True)
    byte = np.maximum(np.where(amax > 0, np.frexp(amax)[1] - 1 + 127, 0) - down, 1)
    scale = np.exp2(byte - 127.0)
    codes = (blocks / scale).astype(np.float32).astype(dtype).astype(np.float64)
    return np.moveaxis((codes * scale).reshape(v.shape), -1, axis)


WIDE = False


def mx_kscale(k):
    if not WIDE:
        return np.ones(k)
    levels = np.array([10, -10, 5, -5, 0])
    if k % 512:
        return np.exp2(np.random.permutation(np.resize(levels, k // 32))).repeat(32)
    a = np.empty((k // 512, 16))
    for p in range(k // 512):
        a[p, :8] = np.random.permutation(np.resize(levels, 8))
        for g in range(8):
            far = levels[np.abs(levels - a[p, g]) >= 10]
            a[p, g + 8] = far[np.random.randint(len(far))]
    return np.exp2(a.ravel()).repeat(32)


def f64(x):
    return np.asarray(x).astype(np.float64)


def striped(idx):
    return np.tile(idx.reshape(-1, 16).T, (8, 1)).astype(np.uint16)


def unstriped(offs):
    return offs[:16].T.reshape(-1).astype(np.int64)


def pack_weight(w):
    k, n = w.shape
    w = f64(np.asarray(w, np.float32).astype(ml_dtypes.bfloat16)).reshape(k // 32, 32, n)
    amax = np.abs(w).max(1)
    byte = np.clip(np.where(amax > 0, np.frexp(amax)[1] - 1 + 127 - 7, 1), 1, 254)
    scaled = (w * np.exp2(127.0 - byte)[:, None, :]).reshape(k, n).astype(np.float32)
    words = np.ascontiguousarray(scaled.reshape(k // 512, 128, 4, n).transpose(0, 1, 3, 2)).astype(ml_dtypes.float8_e4m3fn).view(np.uint8)
    return words, np.ascontiguousarray(byte.astype(np.uint8).reshape(k // 512, 16, n))


def unpack_weight(words, scales):
    g, p, n, _ = words.shape
    vals = np.ascontiguousarray(words).view(ml_dtypes.float8_e4m3fn).astype(np.float64) * np.repeat(np.exp2(scales.astype(np.float64) - 127.0), 8, axis=1)[..., None]
    return vals.transpose(0, 1, 3, 2).reshape(g * 512, n)


def relu(v):
    return np.maximum(v, 0.0)


K, T, S, H, N = 512, 2048, 1024, 512, 128


def setup_inputs():
    n = np.random.standard_normal
    s = mx_kscale(K)[:, None]
    u = mx_kscale(H)
    packed_xT = pack_weight(n((K, T)) * s)
    return {
        "x_words": packed_xT[0],
        "x_scales": packed_xT[1],
        "w1": (n((K, H)) / np.sqrt(K) / s * u).astype(np.float32),
        "w2": (n((H, N)) / np.sqrt(H) / u[:, None]).astype(np.float32),
        "noise": (0.3 * n((H, S)) * u[:, None]).astype(np.float32),
        "obs": (-n((N, 1))).astype(np.float32),
        "offs": striped(np.random.randint(0, T, S)),
    }


def reference(x_words, x_scales, w1, w2, noise, obs, offs):
    xq = unpack_weight(x_words, x_scales)[:, unstriped(offs)]
    h = relu((mxq(f64(w1), 0, "e4m3").T @ xq) + f64(noise))
    dd = (mxq(f64(w2), 0, "e4m3").T @ mxq(h, 0, "e4m3")) + f64(obs)
    return np.exp(-0.5 * ((dd) ** 2))

@@ -1,0 +1,191 @@
+from contextlib import ExitStack
+
+import concourse.mybir as mybir
+
+K, T, S, H, N = 512, 2048, 1024, 512, 128
+FLOPS = 2 * K * H * S + 2 * H * N * S
+
+F32 = mybir.dt.float32
+BF16 = mybir.dt.bfloat16
+I32 = mybir.dt.int32
+U32 = mybir.dt.uint32
+U16 = mybir.dt.uint16
+U8 = mybir.dt.uint8
+FP8X4 = mybir.dt.float8_e4m3fn_x4
+ACT = mybir.ActivationFunctionType
+ALU = mybir.AluOpType
+
+P = 128
+PACK = 4
+CHUNK = 128
+GATHER = 256
+NOISE_COLS = 256
+HALF = 64
+VECTOR_M = 32
+HEAD_COLS = 512
+GROUPS = ((0, 1), (2, 3), (4, 5), (6,), (7,))
+VECTOR_RELU = (6, 7)
+
+
+def tile_picked_ypart_gauss_p_kernel(tc, x_words, x_scales, w1, w2, noise, obs, offs, out):
+    nc = tc.nc
+    with ExitStack() as ctx:
+        keep = ctx.enter_context(tc.tile_pool(name="keep", bufs=1))
+        psum1 = ctx.enter_context(tc.psum_pool(name="psum1", bufs=6))
+        psum2 = ctx.enter_context(tc.psum_pool(name="psum2", bufs=2))
+
+        offsets = keep.tile([P, S // 16], U16, name="offsets")
+        table_scales = keep.tile([P, T], U8, name="table_scales", align_bytes=64)
+        table_words = keep.tile([P, T], U32, name="table_words", align_bytes=64)
+        obs_col = keep.tile([P, 1], F32, name="obs_col")
+
+        nc.vector.memset(table_scales[:].bitcast(I32), 0)
+        nc.sync.dma_start(offsets[:], offs)
+        word_rows = x_words[0].rearrange("p n r -> p (n r)").bitcast(I32)
+        nc.sync.dma_start(table_words[:, 0:HEAD_COLS].bitcast(I32), word_rows[:, 0:HEAD_COLS])
+        for q in range(4):
+            (nc.sync if q < 2 else nc.scalar).dma_start(
+                table_scales[32 * q : 32 * q + 4, :].bitcast(I32),
+                x_scales[0, 4 * q : 4 * q + 4, :].bitcast(I32),
+            )
+        nc.sync.dma_start(table_words[:, HEAD_COLS:T].bitcast(I32), word_rows[:, HEAD_COLS:T])
+
+        w1_rows = w1.rearrange("(p j) c -> p j c", j=PACK)
+        w1_raw = []
+        for half in range(2):
+            raw = keep.tile([P, PACK, H // 2], F32, name="w1_raw%d" % half, align_bytes=64)
+            nc.sync.dma_start(raw[:], w1_rows[:, :, half * (H // 2) : (half + 1) * (H // 2)])
+            w1_raw.append(raw)
+        w2_raw = keep.tile([P, PACK, N], F32, name="w2_raw", align_bytes=64)
+        nc.sync.dma_start(w2_raw[:], w2.rearrange("(p j) n -> p j n", j=PACK))
+        noise_rows = noise.rearrange("(p t) n -> p t n", t=PACK)
+        noise_sb = []
+        for g in range(S // NOISE_COLS):
+            nz = keep.tile([P, PACK, NOISE_COLS], F32, name="noise%d" % g, align_bytes=64)
+            nc.sync.dma_start(nz[:], noise_rows[:, :, g * NOISE_COLS : (g + 1) * NOISE_COLS])
+            noise_sb.append(nz)
+            if g == 1:
+                nc.sync.dma_start(obs_col[:], obs)
+
+        x_scale = keep.tile([P, S], U8, name="x_scale", align_bytes=64)
+        nc.vector.tensor_copy(x_scale[:], table_scales[:].indirect(offsets[:]))
+        x_code = []
+
+        def gather_words(g, tag):
+            codes = keep.tile([P, GATHER], U32, name="x_code%d" % g, tag=tag, align_bytes=64)
+            nc.vector.tensor_copy(
+                codes[:], table_words[:].indirect(offsets[:, g * GATHER // 16 : (g + 1) * GATHER // 16])
+            )
+            x_code.append(codes)
+
+        for g in range(3):
+            gather_words(g, "x_code%d" % g)
+
+        w1_bf = keep.tile([P, PACK, P, PACK], BF16, name="w1_bf", tag="w1_bf", align_bytes=64)
+        w1_dst = w1_bf[:].rearrange("p t m j -> p m j t")
+        w1_src = [raw[:].rearrange("p j (m t) -> p m j t", t=PACK) for raw in w1_raw]
+        nc.scalar.activation(w1_dst[:, 0:HALF], w1_src[0], ACT.Copy)
+        nc.vector.tensor_copy(w1_dst[:, HALF : HALF + VECTOR_M], w1_src[1][:, 0:VECTOR_M])
+        nc.scalar.activation(w1_dst[:, HALF + VECTOR_M : P], w1_src[1][:, VECTOR_M:HALF], ACT.Copy)
+        w1_code = keep.tile([P, H], U32, name="w1_code", align_bytes=64)
+        w1_scale = keep.tile([P, H], U8, name="w1_scale", align_bytes=64)
+        w1_flat = w1_bf[:].rearrange("p t m j -> p (t m j)")
+        for cols in (slice(0, 2 * P), slice(2 * P, 3 * P), slice(3 * P, 4 * P)):
+            nc.vector.quantize_mx(
+                out=w1_code[:, cols].bitcast(FP8X4),
+                scales=w1_scale[:, cols],
+                in_=w1_flat[:, cols.start * PACK : cols.stop * PACK],
+            )
+        gather_words(3, "w1_bf")
+
+        w2_bf = keep.tile([P, N * PACK], BF16, name="w2_bf", align_bytes=64)
+        nc.scalar.activation(
+            w2_bf[:].rearrange("p (c i j) -> p c j i", i=2, j=PACK),
+            w2_raw[:].rearrange("p j (c i) -> p c j i", i=2),
+            ACT.Copy,
+        )
+        w2_code = keep.tile([P, N], U32, name="w2_code", align_bytes=64)
+        w2_scale = keep.tile([P, N], U8, name="w2_scale", align_bytes=64)
+        nc.vector.quantize_mx(out=w2_code[:].bitcast(FP8X4), scales=w2_scale[:], in_=w2_bf[:])
+
+        pre = keep.tile([P, S * PACK], BF16, name="pre", align_bytes=64)
+        hid = keep.tile([P, S * PACK], BF16, name="hid", align_bytes=64)
+        h_code = keep.tile([P, S], U32, name="h_code", align_bytes=64)
+        h_scale = keep.tile([P, S], U8, name="h_scale", align_bytes=64)
+        sq = keep.tile([P, S], F32, name="sq", align_bytes=64)
+        res = keep.tile([P, S], F32, name="res", align_bytes=64)
+
+        def first_layer(c):
+            cols = slice(c * CHUNK, (c + 1) * CHUNK)
+            xg, x0 = divmod(c * CHUNK, GATHER)
+            bank = psum1.tile([P, PACK, CHUNK], F32, name="bank")
+            for t in range(PACK):
+                tcols = slice(t * P, (t + 1) * P)
+                nc.tensor.matmul_mx(
+                    out=bank[:, t, :],
+                    lhsT=w1_code[:, tcols].bitcast(FP8X4),
+                    lhsT_scale=w1_scale[:, tcols],
+                    rhs=x_code[xg][:, x0 : x0 + CHUNK].bitcast(FP8X4),
+                    rhs_scale=x_scale[:, cols],
+                    start=True,
+                    stop=True,
+                )
+            g, n0 = divmod(c * CHUNK, NOISE_COLS)
+            span = slice(c * CHUNK * PACK, (c + 1) * CHUNK * PACK)
+            nc.vector.tensor_tensor(
+                pre[:, span].rearrange("p (c i t) -> p c t i", i=2, t=PACK),
+                bank[:].rearrange("p t (c i) -> p c t i", i=2),
+                noise_sb[g][:, :, n0 : n0 + CHUNK].rearrange("p t (c i) -> p c t i", i=2),
+                ALU.add,
+            )
+
+        def rectify(c):
+            span = slice(c * CHUNK * PACK, (c + 1) * CHUNK * PACK)
+            if c in VECTOR_RELU:
+                nc.vector.tensor_scalar_max(hid[:, span], pre[:, span], 0.0)
+            else:
+                nc.scalar.activation(hid[:, span], pre[:, span], ACT.Relu)
+
+        def second_layer(group):
+            cols = slice(group[0] * CHUNK, (group[-1] + 1) * CHUNK)
+            width = len(group) * CHUNK
+            nc.vector.quantize_mx(
+                out=h_code[:, cols].bitcast(FP8X4),
+                scales=h_scale[:, cols],
+                in_=hid[:, cols.start * PACK : cols.stop * PACK],
+            )
+            acc = psum2.tile([P, 2 * CHUNK], F32, name="acc")
+            nc.tensor.matmul_mx(
+                out=acc[:, 0:width],
+                lhsT=w2_code[:].bitcast(FP8X4),
+                lhsT_scale=w2_scale[:],
+                rhs=h_code[:, cols].bitcast(FP8X4),
+                rhs_scale=h_scale[:, cols],
+                start=True,
+                stop=True,
+            )
+            nc.scalar.activation(sq[:, cols], acc[:, 0:width], ACT.Square, bias=obs_col[:])
+            nc.scalar.activation(res[:, cols], sq[:, cols], ACT.Exp, scale=-0.5)
+            nc.sync.dma_start(out[:, cols], res[:, cols])
+
+        first_layer(0)
+        rectify(0)
+        first_layer(1)
+        rectify(1)
+        first_layer(2)
+        rectify(2)
+        second_layer(GROUPS[0])
+        first_layer(3)
+        rectify(3)
+        first_layer(4)
+        rectify(4)
+        second_layer(GROUPS[1])
+        first_layer(5)
+        rectify(5)
+        first_layer(6)
+        first_layer(7)
+        second_layer(GROUPS[2])
+        rectify(6)
+        rectify(7)
+        second_layer(GROUPS[3])
+        second_layer(GROUPS[4])

@@ -21,8 +21,7 @@ CHUNK = 128
 GATHER = 256
 NOISE_COLS = 256
 HALF = 64
-VECTOR_M = 32
-HEAD_COLS = 512
+VECTOR_M = 40
 GROUPS = ((0, 1), (2, 3), (4, 5), (6,), (7,))
 VECTOR_RELU = (6, 7)
 
@@ -31,24 +30,22 @@ def tile_picked_ypart_gauss_p_kernel(tc, x_words, x_scales, w1, w2, noise, obs, 
     nc = tc.nc
     with ExitStack() as ctx:
         keep = ctx.enter_context(tc.tile_pool(name="keep", bufs=1))
-        psum1 = ctx.enter_context(tc.psum_pool(name="psum1", bufs=6))
-        psum2 = ctx.enter_context(tc.psum_pool(name="psum2", bufs=2))
+        psum1 = ctx.enter_context(tc.psum_pool(name="psum1", bufs=5))
+        psum2 = ctx.enter_context(tc.psum_pool(name="psum2", bufs=3))
 
         offsets = keep.tile([P, S // 16], U16, name="offsets")
-        table_scales = keep.tile([P, T], U8, name="table_scales", align_bytes=64)
+        table_scales = keep.tile([P, T], U8, name="table_scales", tag="table_scales", align_bytes=64)
         table_words = keep.tile([P, T], U32, name="table_words", align_bytes=64)
-        obs_col = keep.tile([P, 1], F32, name="obs_col")
 
-        nc.vector.memset(table_scales[:].bitcast(I32), 0)
+        picked_scales = keep.tile([P, S], U8, name="picked_scales", align_bytes=64)
+        x_scale = keep.tile([P, S], U8, name="x_scale", align_bytes=64)
+
         nc.sync.dma_start(offsets[:], offs)
-        word_rows = x_words[0].rearrange("p n r -> p (n r)").bitcast(I32)
-        nc.sync.dma_start(table_words[:, 0:HEAD_COLS].bitcast(I32), word_rows[:, 0:HEAD_COLS])
-        for q in range(4):
-            (nc.sync if q < 2 else nc.scalar).dma_start(
-                table_scales[32 * q : 32 * q + 4, :].bitcast(I32),
-                x_scales[0, 4 * q : 4 * q + 4, :].bitcast(I32),
-            )
-        nc.sync.dma_start(table_words[:, HEAD_COLS:T].bitcast(I32), word_rows[:, HEAD_COLS:T])
+        nc.scalar.dma_start(table_scales[16:32, :].bitcast(I32), x_scales[0].bitcast(I32))
+        nc.sync.dma_start(table_words[:].bitcast(I32), x_words[0].rearrange("p n r -> p (n r)").bitcast(I32))
+        for rows in (slice(0, 16), slice(32, 64), slice(64, P)):
+            nc.vector.memset(table_scales[rows, :].bitcast(I32), 0)
+        nc.vector.memset(x_scale[:].bitcast(I32), 0)
 
         w1_rows = w1.rearrange("(p j) c -> p j c", j=PACK)
         w1_raw = []
@@ -56,19 +53,28 @@ def tile_picked_ypart_gauss_p_kernel(tc, x_words, x_scales, w1, w2, noise, obs, 
             raw = keep.tile([P, PACK, H // 2], F32, name="w1_raw%d" % half, align_bytes=64)
             nc.sync.dma_start(raw[:], w1_rows[:, :, half * (H // 2) : (half + 1) * (H // 2)])
             w1_raw.append(raw)
+        noise_rows = noise.rearrange("(p t) n -> p t n", t=PACK)
         w2_raw = keep.tile([P, PACK, N], F32, name="w2_raw", align_bytes=64)
         nc.sync.dma_start(w2_raw[:], w2.rearrange("(p j) n -> p j n", j=PACK))
-        noise_rows = noise.rearrange("(p t) n -> p t n", t=PACK)
+
+        nc.vector.tensor_copy(picked_scales[:], table_scales[:].indirect(offsets[:]))
+        for q in range(4):
+            nc.sync.dma_start(
+                x_scale[32 * q : 32 * q + 4, :].bitcast(I32),
+                picked_scales[16 + 4 * q : 16 + 4 * q + 4, :].bitcast(I32),
+            )
+
+        piece = PACK * NOISE_COLS
+        late = keep.tile([P, 4 * piece + 8], F32, name="late", tag="table_scales", align_bytes=64)
+        obs_col = late[:, 4 * piece : 4 * piece + 1]
         noise_sb = []
         for g in range(S // NOISE_COLS):
-            nz = keep.tile([P, PACK, NOISE_COLS], F32, name="noise%d" % g, align_bytes=64)
-            nc.sync.dma_start(nz[:], noise_rows[:, :, g * NOISE_COLS : (g + 1) * NOISE_COLS])
+            nz = late[:, g * piece : (g + 1) * piece].rearrange("p (t n) -> p t n", t=PACK)
+            nc.sync.dma_start(nz, noise_rows[:, :, g * NOISE_COLS : (g + 1) * NOISE_COLS])
             noise_sb.append(nz)
             if g == 1:
-                nc.sync.dma_start(obs_col[:], obs)
+                nc.sync.dma_start(obs_col, obs)
 
-        x_scale = keep.tile([P, S], U8, name="x_scale", align_bytes=64)
-        nc.vector.tensor_copy(x_scale[:], table_scales[:].indirect(offsets[:]))
         x_code = []
 
         def gather_words(g, tag):
@@ -164,7 +170,7 @@ def tile_picked_ypart_gauss_p_kernel(tc, x_words, x_scales, w1, w2, noise, obs, 
                 start=True,
                 stop=True,
             )
-            nc.scalar.activation(sq[:, cols], acc[:, 0:width], ACT.Square, bias=obs_col[:])
+            nc.scalar.activation(sq[:, cols], acc[:, 0:width], ACT.Square, bias=obs_col)
             nc.scalar.activation(res[:, cols], sq[:, cols], ACT.Exp, scale=-0.5)
             nc.sync.dma_start(out[:, cols], res[:, cols])
 

@@ -19,9 +19,9 @@ P = 128
 PACK = 4
 CHUNK = 128
 GATHER = 256
-NOISE_COLS = 256
+NOISE_PIECES = (128,) * 8
 HALF = 64
-VECTOR_M = 40
+VECTOR_M = 48
 GROUPS = ((0, 1), (2, 3), (4, 5), (6,), (7,))
 VECTOR_RELU = (6, 7)
 
@@ -54,8 +54,8 @@ def tile_picked_ypart_gauss_p_kernel(tc, x_words, x_scales, w1, w2, noise, obs, 
             nc.sync.dma_start(raw[:], w1_rows[:, :, half * (H // 2) : (half + 1) * (H // 2)])
             w1_raw.append(raw)
         noise_rows = noise.rearrange("(p t) n -> p t n", t=PACK)
-        w2_raw = keep.tile([P, PACK, N], F32, name="w2_raw", align_bytes=64)
-        nc.sync.dma_start(w2_raw[:], w2.rearrange("(p j) n -> p j n", j=PACK))
+        noise_head = keep.tile([P, PACK, CHUNK], F32, name="noise_head", align_bytes=64)
+        nc.sync.dma_start(noise_head[:], noise_rows[:, :, 0:CHUNK])
 
         nc.vector.tensor_copy(picked_scales[:], table_scales[:].indirect(offsets[:]))
         for q in range(4):
@@ -64,16 +64,19 @@ def tile_picked_ypart_gauss_p_kernel(tc, x_words, x_scales, w1, w2, noise, obs, 
                 picked_scales[16 + 4 * q : 16 + 4 * q + 4, :].bitcast(I32),
             )
 
-        piece = PACK * NOISE_COLS
-        late = keep.tile([P, 4 * piece + 8], F32, name="late", tag="table_scales", align_bytes=64)
-        obs_col = late[:, 4 * piece : 4 * piece + 1]
-        noise_sb = []
-        for g in range(S // NOISE_COLS):
-            nz = late[:, g * piece : (g + 1) * piece].rearrange("p (t n) -> p t n", t=PACK)
-            nc.sync.dma_start(nz, noise_rows[:, :, g * NOISE_COLS : (g + 1) * NOISE_COLS])
-            noise_sb.append(nz)
-            if g == 1:
+        late = keep.tile([P, PACK * S + 8], F32, name="late", tag="table_scales", align_bytes=64)
+        w2_raw = late[:, 0 : PACK * N].rearrange("p (j n) -> p j n", j=PACK)
+        obs_col = late[:, PACK * S : PACK * S + 1]
+        nc.sync.dma_start(w2_raw, w2.rearrange("(p j) n -> p j n", j=PACK))
+        noise_chunk = [noise_head[:]]
+        n0 = CHUNK
+        for width in NOISE_PIECES[1:]:
+            nz = late[:, PACK * n0 : PACK * (n0 + width)].rearrange("p (t n) -> p t n", t=PACK)
+            nc.sync.dma_start(nz, noise_rows[:, :, n0 : n0 + width])
+            noise_chunk.extend(nz[:, :, c0 : c0 + CHUNK] for c0 in range(0, width, CHUNK))
+            if n0 == 2 * CHUNK:
                 nc.sync.dma_start(obs_col, obs)
+            n0 = n0 + width
 
         x_code = []
 
@@ -96,7 +99,7 @@ def tile_picked_ypart_gauss_p_kernel(tc, x_words, x_scales, w1, w2, noise, obs, 
         w1_code = keep.tile([P, H], U32, name="w1_code", align_bytes=64)
         w1_scale = keep.tile([P, H], U8, name="w1_scale", align_bytes=64)
         w1_flat = w1_bf[:].rearrange("p t m j -> p (t m j)")
-        for cols in (slice(0, 2 * P), slice(2 * P, 3 * P), slice(3 * P, 4 * P)):
+        for cols in [slice(t * P, (t + 1) * P) for t in range(PACK)]:
             nc.vector.quantize_mx(
                 out=w1_code[:, cols].bitcast(FP8X4),
                 scales=w1_scale[:, cols],
@@ -107,7 +110,7 @@ def tile_picked_ypart_gauss_p_kernel(tc, x_words, x_scales, w1, w2, noise, obs, 
         w2_bf = keep.tile([P, N * PACK], BF16, name="w2_bf", align_bytes=64)
         nc.scalar.activation(
             w2_bf[:].rearrange("p (c i j) -> p c j i", i=2, j=PACK),
-            w2_raw[:].rearrange("p j (c i) -> p c j i", i=2),
+            w2_raw.rearrange("p j (c i) -> p c j i", i=2),
             ACT.Copy,
         )
         w2_code = keep.tile([P, N], U32, name="w2_code", align_bytes=64)
@@ -136,12 +139,11 @@ def tile_picked_ypart_gauss_p_kernel(tc, x_words, x_scales, w1, w2, noise, obs, 
                     start=True,
                     stop=True,
                 )
-            g, n0 = divmod(c * CHUNK, NOISE_COLS)
             span = slice(c * CHUNK * PACK, (c + 1) * CHUNK * PACK)
             nc.vector.tensor_tensor(
                 pre[:, span].rearrange("p (c i t) -> p c t i", i=2, t=PACK),
                 bank[:].rearrange("p t (c i) -> p c t i", i=2),
-                noise_sb[g][:, :, n0 : n0 + CHUNK].rearrange("p t (c i) -> p c t i", i=2),
+                noise_chunk[c].rearrange("p t (c i) -> p c t i", i=2),
                 ALU.add,
             )
 

@@ -18,12 +18,16 @@ ALU = mybir.AluOpType
 P = 128
 PACK = 4
 CHUNK = 128
-GATHER = 256
-NOISE_PIECES = (128,) * 8
+W1_PIECES = 4
+PIECE_M = P // W1_PIECES
 HALF = 64
-VECTOR_M = 48
-GROUPS = ((0, 1), (2, 3), (4, 5), (6,), (7,))
-VECTOR_RELU = (6, 7)
+VECTOR_M = 20
+SCALE_ROW = 112
+NOISE_PIECES = (128, 128, 256, 256, 256)
+GATHERS = (768, 256)
+ADDS = tuple((c * CHUNK, (c + 1) * CHUNK) for c in range(8))
+GROUPS = ((0, 256), (256, 512), (512, 768), (768, 896), (896, 1024))
+VECTOR_RELU_FROM = 768
 
 
 def tile_picked_ypart_gauss_p_kernel(tc, x_words, x_scales, w1, w2, noise, obs, offs, out):
@@ -41,71 +45,84 @@ def tile_picked_ypart_gauss_p_kernel(tc, x_words, x_scales, w1, w2, noise, obs, 
         x_scale = keep.tile([P, S], U8, name="x_scale", align_bytes=64)
 
         nc.sync.dma_start(offsets[:], offs)
-        nc.scalar.dma_start(table_scales[16:32, :].bitcast(I32), x_scales[0].bitcast(I32))
+        nc.scalar.dma_start(table_scales[SCALE_ROW:P, :].bitcast(I32), x_scales[0].bitcast(I32))
         nc.sync.dma_start(table_words[:].bitcast(I32), x_words[0].rearrange("p n r -> p (n r)").bitcast(I32))
-        for rows in (slice(0, 16), slice(32, 64), slice(64, P)):
-            nc.vector.memset(table_scales[rows, :].bitcast(I32), 0)
+        nc.vector.memset(table_scales[0:SCALE_ROW, :].bitcast(I32), 0)
         nc.vector.memset(x_scale[:].bitcast(I32), 0)
 
         w1_rows = w1.rearrange("(p j) c -> p j c", j=PACK)
         w1_raw = []
-        for half in range(2):
-            raw = keep.tile([P, PACK, H // 2], F32, name="w1_raw%d" % half, align_bytes=64)
-            nc.sync.dma_start(raw[:], w1_rows[:, :, half * (H // 2) : (half + 1) * (H // 2)])
+        for piece in range(W1_PIECES):
+            raw = keep.tile([P, PACK, PIECE_M * PACK], F32, name="w1_raw%d" % piece, align_bytes=64)
+            nc.sync.dma_start(raw[:], w1_rows[:, :, piece * PIECE_M * PACK : (piece + 1) * PIECE_M * PACK])
             w1_raw.append(raw)
         noise_rows = noise.rearrange("(p t) n -> p t n", t=PACK)
-        noise_head = keep.tile([P, PACK, CHUNK], F32, name="noise_head", align_bytes=64)
-        nc.sync.dma_start(noise_head[:], noise_rows[:, :, 0:CHUNK])
+        noise_head = keep.tile([P, PACK, NOISE_PIECES[0]], F32, name="noise_head", align_bytes=64)
+        nc.sync.dma_start(noise_head[:], noise_rows[:, :, 0 : NOISE_PIECES[0]])
 
         nc.vector.tensor_copy(picked_scales[:], table_scales[:].indirect(offsets[:]))
         for q in range(4):
             nc.sync.dma_start(
                 x_scale[32 * q : 32 * q + 4, :].bitcast(I32),
-                picked_scales[16 + 4 * q : 16 + 4 * q + 4, :].bitcast(I32),
+                picked_scales[SCALE_ROW + 4 * q : SCALE_ROW + 4 * q + 4, :].bitcast(I32),
             )
 
-        late = keep.tile([P, PACK * S + 8], F32, name="late", tag="table_scales", align_bytes=64)
-        w2_raw = late[:, 0 : PACK * N].rearrange("p (j n) -> p j n", j=PACK)
-        obs_col = late[:, PACK * S : PACK * S + 1]
-        nc.sync.dma_start(w2_raw, w2.rearrange("(p j) n -> p j n", j=PACK))
-        noise_chunk = [noise_head[:]]
-        n0 = CHUNK
-        for width in NOISE_PIECES[1:]:
-            nz = late[:, PACK * n0 : PACK * (n0 + width)].rearrange("p (t n) -> p t n", t=PACK)
-            nc.sync.dma_start(nz, noise_rows[:, :, n0 : n0 + width])
+        late = keep.tile([P, PACK * (S + N) + 8], F32, name="late", tag="table_scales", align_bytes=64)
+        w2_raw = late[:, PACK * S : PACK * (S + N)].rearrange("p (j n) -> p j n", j=PACK)
+        obs_col = late[:, PACK * (S + N) : PACK * (S + N) + 1]
+        noise_chunk = []
+        n0 = 0
+        for piece, width in enumerate(NOISE_PIECES):
+            if piece == 0:
+                nz = noise_head[:]
+            else:
+                nz = late[:, PACK * n0 : PACK * (n0 + width)].rearrange("p (t n) -> p t n", t=PACK)
+                nc.sync.dma_start(nz, noise_rows[:, :, n0 : n0 + width])
             noise_chunk.extend(nz[:, :, c0 : c0 + CHUNK] for c0 in range(0, width, CHUNK))
-            if n0 == 2 * CHUNK:
+            if piece == 0:
+                nc.sync.dma_start(w2_raw, w2.rearrange("(p j) n -> p j n", j=PACK))
+            if piece == 2:
                 nc.sync.dma_start(obs_col, obs)
             n0 = n0 + width
 
         x_code = []
 
-        def gather_words(g, tag):
-            codes = keep.tile([P, GATHER], U32, name="x_code%d" % g, tag=tag, align_bytes=64)
-            nc.vector.tensor_copy(
-                codes[:], table_words[:].indirect(offsets[:, g * GATHER // 16 : (g + 1) * GATHER // 16])
-            )
-            x_code.append(codes)
+        def gather_words(j0, width, tag):
+            codes = keep.tile([P, width], U32, name="x_code%d" % j0, tag=tag, align_bytes=64)
+            nc.vector.tensor_copy(codes[:], table_words[:].indirect(offsets[:, j0 // 16 : (j0 + width) // 16]))
+            x_code.extend(codes[:, c0 : c0 + CHUNK] for c0 in range(0, width, CHUNK))
 
-        for g in range(3):
-            gather_words(g, "x_code%d" % g)
+        j0 = 0
+        for width in GATHERS[:-1]:
+            gather_words(j0, width, "x_code%d" % j0)
+            j0 = j0 + width
 
         w1_bf = keep.tile([P, PACK, P, PACK], BF16, name="w1_bf", tag="w1_bf", align_bytes=64)
         w1_dst = w1_bf[:].rearrange("p t m j -> p m j t")
         w1_src = [raw[:].rearrange("p j (m t) -> p m j t", t=PACK) for raw in w1_raw]
-        nc.scalar.activation(w1_dst[:, 0:HALF], w1_src[0], ACT.Copy)
-        nc.vector.tensor_copy(w1_dst[:, HALF : HALF + VECTOR_M], w1_src[1][:, 0:VECTOR_M])
-        nc.scalar.activation(w1_dst[:, HALF + VECTOR_M : P], w1_src[1][:, VECTOR_M:HALF], ACT.Copy)
         w1_code = keep.tile([P, H], U32, name="w1_code", align_bytes=64)
         w1_scale = keep.tile([P, H], U8, name="w1_scale", align_bytes=64)
         w1_flat = w1_bf[:].rearrange("p t m j -> p (t m j)")
-        for cols in [slice(t * P, (t + 1) * P) for t in range(PACK)]:
-            nc.vector.quantize_mx(
-                out=w1_code[:, cols].bitcast(FP8X4),
-                scales=w1_scale[:, cols],
-                in_=w1_flat[:, cols.start * PACK : cols.stop * PACK],
-            )
-        gather_words(3, "w1_bf")
+
+        def quantize_w1_half(half):
+            for t in range(PACK):
+                c0 = t * P + half * HALF
+                nc.vector.quantize_mx(
+                    out=w1_code[:, c0 : c0 + HALF].bitcast(FP8X4),
+                    scales=w1_scale[:, c0 : c0 + HALF],
+                    in_=w1_flat[:, c0 * PACK : (c0 + HALF) * PACK],
+                )
+
+        for piece in range(W1_PIECES):
+            m0 = piece * PIECE_M
+            if piece < W1_PIECES - 1:
+                nc.scalar.activation(w1_dst[:, m0 : m0 + PIECE_M], w1_src[piece], ACT.Copy)
+            else:
+                nc.vector.tensor_copy(w1_dst[:, m0 : m0 + VECTOR_M], w1_src[piece][:, 0:VECTOR_M])
+                nc.scalar.activation(w1_dst[:, m0 + VECTOR_M : P], w1_src[piece][:, VECTOR_M:PIECE_M], ACT.Copy)
+            if m0 + PIECE_M in (HALF, P):
+                quantize_w1_half(m0 // HALF)
+        gather_words(j0, GATHERS[-1], "w1_bf")
 
         w2_bf = keep.tile([P, N * PACK], BF16, name="w2_bf", align_bytes=64)
         nc.scalar.activation(
@@ -124,9 +141,10 @@ def tile_picked_ypart_gauss_p_kernel(tc, x_words, x_scales, w1, w2, noise, obs, 
         sq = keep.tile([P, S], F32, name="sq", align_bytes=64)
         res = keep.tile([P, S], F32, name="res", align_bytes=64)
 
+        banks = {}
+        accs = {}
+
         def first_layer(c):
-            cols = slice(c * CHUNK, (c + 1) * CHUNK)
-            xg, x0 = divmod(c * CHUNK, GATHER)
             bank = psum1.tile([P, PACK, CHUNK], F32, name="bank")
             for t in range(PACK):
                 tcols = slice(t * P, (t + 1) * P)
@@ -134,37 +152,45 @@ def tile_picked_ypart_gauss_p_kernel(tc, x_words, x_scales, w1, w2, noise, obs, 
                     out=bank[:, t, :],
                     lhsT=w1_code[:, tcols].bitcast(FP8X4),
                     lhsT_scale=w1_scale[:, tcols],
-                    rhs=x_code[xg][:, x0 : x0 + CHUNK].bitcast(FP8X4),
-                    rhs_scale=x_scale[:, cols],
+                    rhs=x_code[c].bitcast(FP8X4),
+                    rhs_scale=x_scale[:, c * CHUNK : (c + 1) * CHUNK],
                     start=True,
                     stop=True,
                 )
-            span = slice(c * CHUNK * PACK, (c + 1) * CHUNK * PACK)
+            banks[c] = bank
+
+        def add_noise(a):
+            j0, j1 = ADDS[a]
+            c = j0 // CHUNK
+            if j0 % CHUNK == 0:
+                first_layer(c)
+            inner = slice(j0 - c * CHUNK, j1 - c * CHUNK)
             nc.vector.tensor_tensor(
-                pre[:, span].rearrange("p (c i t) -> p c t i", i=2, t=PACK),
-                bank[:].rearrange("p t (c i) -> p c t i", i=2),
-                noise_chunk[c].rearrange("p t (c i) -> p c t i", i=2),
+                pre[:, j0 * PACK : j1 * PACK].rearrange("p (c i t) -> p c t i", i=2, t=PACK),
+                banks[c][:, :, inner].rearrange("p t (c i) -> p c t i", i=2),
+                noise_chunk[c][:, :, inner].rearrange("p t (c i) -> p c t i", i=2),
                 ALU.add,
             )
 
-        def rectify(c):
-            span = slice(c * CHUNK * PACK, (c + 1) * CHUNK * PACK)
-            if c in VECTOR_RELU:
+        def rectify(a):
+            j0, j1 = ADDS[a]
+            span = slice(j0 * PACK, j1 * PACK)
+            if j0 >= VECTOR_RELU_FROM:
                 nc.vector.tensor_scalar_max(hid[:, span], pre[:, span], 0.0)
             else:
                 nc.scalar.activation(hid[:, span], pre[:, span], ACT.Relu)
 
-        def second_layer(group):
-            cols = slice(group[0] * CHUNK, (group[-1] + 1) * CHUNK)
-            width = len(group) * CHUNK
+        def second_layer(g):
+            j0, j1 = GROUPS[g]
+            cols = slice(j0, j1)
             nc.vector.quantize_mx(
                 out=h_code[:, cols].bitcast(FP8X4),
                 scales=h_scale[:, cols],
-                in_=hid[:, cols.start * PACK : cols.stop * PACK],
+                in_=hid[:, j0 * PACK : j1 * PACK],
             )
-            acc = psum2.tile([P, 2 * CHUNK], F32, name="acc")
+            acc = psum2.tile([P, 256], F32, name="acc")
             nc.tensor.matmul_mx(
-                out=acc[:, 0:width],
+                out=acc[:, 0 : j1 - j0],
                 lhsT=w2_code[:].bitcast(FP8X4),
                 lhsT_scale=w2_scale[:],
                 rhs=h_code[:, cols].bitcast(FP8X4),
@@ -172,28 +198,39 @@ def tile_picked_ypart_gauss_p_kernel(tc, x_words, x_scales, w1, w2, noise, obs, 
                 start=True,
                 stop=True,
             )
-            nc.scalar.activation(sq[:, cols], acc[:, 0:width], ACT.Square, bias=obs_col)
-            nc.scalar.activation(res[:, cols], sq[:, cols], ACT.Exp, scale=-0.5)
+            accs[g] = acc
+
+        def likelihood(g):
+            j0, j1 = GROUPS[g]
+            cols = slice(j0, j1)
+            squares = sq[:, cols]
+            nc.scalar.activation(squares, accs[g][:, 0 : j1 - j0], ACT.Square, bias=obs_col)
+            nc.scalar.activation(res[:, cols], squares, ACT.Exp, scale=-0.5)
             nc.sync.dma_start(out[:, cols], res[:, cols])
 
-        first_layer(0)
+        add_noise(0)
         rectify(0)
-        first_layer(1)
+        add_noise(1)
         rectify(1)
-        first_layer(2)
+        add_noise(2)
         rectify(2)
-        second_layer(GROUPS[0])
-        first_layer(3)
+        add_noise(3)
         rectify(3)
-        first_layer(4)
+        second_layer(0)
+        add_noise(4)
         rectify(4)
-        second_layer(GROUPS[1])
-        first_layer(5)
+        likelihood(0)
+        add_noise(5)
         rectify(5)
-        first_layer(6)
-        first_layer(7)
-        second_layer(GROUPS[2])
+        second_layer(1)
+        add_noise(6)
+        likelihood(1)
+        second_layer(2)
         rectify(6)
+        add_noise(7)
         rectify(7)
-        second_layer(GROUPS[3])
-        second_layer(GROUPS[4])
+        second_layer(3)
+        second_layer(4)
+        likelihood(2)
+        likelihood(3)
+        likelihood(4)

@@ -18,12 +18,9 @@ ALU = mybir.AluOpType
 P = 128
 PACK = 4
 CHUNK = 128
-W1_PIECES = 4
-PIECE_M = P // W1_PIECES
-HALF = 64
-VECTOR_M = 20
+VECTOR_M = 44
 SCALE_ROW = 112
-NOISE_PIECES = (128, 128, 256, 256, 256)
+NOISE_PIECES = (256,) * 4
 GATHERS = (768, 256)
 ADDS = tuple((c * CHUNK, (c + 1) * CHUNK) for c in range(8))
 GROUPS = ((0, 256), (256, 512), (512, 768), (768, 896), (896, 1024))
@@ -50,15 +47,11 @@ def tile_picked_ypart_gauss_p_kernel(tc, x_words, x_scales, w1, w2, noise, obs, 
         nc.vector.memset(table_scales[0:SCALE_ROW, :].bitcast(I32), 0)
         nc.vector.memset(x_scale[:].bitcast(I32), 0)
 
-        w1_rows = w1.rearrange("(p j) c -> p j c", j=PACK)
-        w1_raw = []
-        for piece in range(W1_PIECES):
-            raw = keep.tile([P, PACK, PIECE_M * PACK], F32, name="w1_raw%d" % piece, align_bytes=64)
-            nc.sync.dma_start(raw[:], w1_rows[:, :, piece * PIECE_M * PACK : (piece + 1) * PIECE_M * PACK])
-            w1_raw.append(raw)
+        w1_raw = keep.tile([P, PACK, H], F32, name="w1_raw", align_bytes=64)
+        nc.sync.dma_start(w1_raw[:], w1.rearrange("(p j) c -> p j c", j=PACK))
+        w2_raw = keep.tile([P, PACK, N], F32, name="w2_raw", align_bytes=64)
+        nc.sync.dma_start(w2_raw[:], w2.rearrange("(p j) n -> p j n", j=PACK))
         noise_rows = noise.rearrange("(p t) n -> p t n", t=PACK)
-        noise_head = keep.tile([P, PACK, NOISE_PIECES[0]], F32, name="noise_head", align_bytes=64)
-        nc.sync.dma_start(noise_head[:], noise_rows[:, :, 0 : NOISE_PIECES[0]])
 
         nc.vector.tensor_copy(picked_scales[:], table_scales[:].indirect(offsets[:]))
         for q in range(4):
@@ -67,21 +60,15 @@ def tile_picked_ypart_gauss_p_kernel(tc, x_words, x_scales, w1, w2, noise, obs, 
                 picked_scales[SCALE_ROW + 4 * q : SCALE_ROW + 4 * q + 4, :].bitcast(I32),
             )
 
-        late = keep.tile([P, PACK * (S + N) + 8], F32, name="late", tag="table_scales", align_bytes=64)
-        w2_raw = late[:, PACK * S : PACK * (S + N)].rearrange("p (j n) -> p j n", j=PACK)
-        obs_col = late[:, PACK * (S + N) : PACK * (S + N) + 1]
+        late = keep.tile([P, PACK * S + 8], F32, name="late", tag="table_scales", align_bytes=64)
+        obs_col = late[:, PACK * S : PACK * S + 1]
         noise_chunk = []
         n0 = 0
         for piece, width in enumerate(NOISE_PIECES):
-            if piece == 0:
-                nz = noise_head[:]
-            else:
-                nz = late[:, PACK * n0 : PACK * (n0 + width)].rearrange("p (t n) -> p t n", t=PACK)
-                nc.sync.dma_start(nz, noise_rows[:, :, n0 : n0 + width])
+            nz = late[:, PACK * n0 : PACK * (n0 + width)].rearrange("p (t n) -> p t n", t=PACK)
+            nc.sync.dma_start(nz, noise_rows[:, :, n0 : n0 + width])
             noise_chunk.extend(nz[:, :, c0 : c0 + CHUNK] for c0 in range(0, width, CHUNK))
             if piece == 0:
-                nc.sync.dma_start(w2_raw, w2.rearrange("(p j) n -> p j n", j=PACK))
-            if piece == 2:
                 nc.sync.dma_start(obs_col, obs)
             n0 = n0 + width
 
@@ -99,35 +86,26 @@ def tile_picked_ypart_gauss_p_kernel(tc, x_words, x_scales, w1, w2, noise, obs, 
 
         w1_bf = keep.tile([P, PACK, P, PACK], BF16, name="w1_bf", tag="w1_bf", align_bytes=64)
         w1_dst = w1_bf[:].rearrange("p t m j -> p m j t")
-        w1_src = [raw[:].rearrange("p j (m t) -> p m j t", t=PACK) for raw in w1_raw]
+        w1_src = w1_raw[:].rearrange("p j (m t) -> p m j t", t=PACK)
         w1_code = keep.tile([P, H], U32, name="w1_code", align_bytes=64)
         w1_scale = keep.tile([P, H], U8, name="w1_scale", align_bytes=64)
         w1_flat = w1_bf[:].rearrange("p t m j -> p (t m j)")
 
-        def quantize_w1_half(half):
-            for t in range(PACK):
-                c0 = t * P + half * HALF
-                nc.vector.quantize_mx(
-                    out=w1_code[:, c0 : c0 + HALF].bitcast(FP8X4),
-                    scales=w1_scale[:, c0 : c0 + HALF],
-                    in_=w1_flat[:, c0 * PACK : (c0 + HALF) * PACK],
-                )
-
-        for piece in range(W1_PIECES):
-            m0 = piece * PIECE_M
-            if piece < W1_PIECES - 1:
-                nc.scalar.activation(w1_dst[:, m0 : m0 + PIECE_M], w1_src[piece], ACT.Copy)
-            else:
-                nc.vector.tensor_copy(w1_dst[:, m0 : m0 + VECTOR_M], w1_src[piece][:, 0:VECTOR_M])
-                nc.scalar.activation(w1_dst[:, m0 + VECTOR_M : P], w1_src[piece][:, VECTOR_M:PIECE_M], ACT.Copy)
-            if m0 + PIECE_M in (HALF, P):
-                quantize_w1_half(m0 // HALF)
+        nc.scalar.activation(w1_dst[:, VECTOR_M:P, :, 2:4], w1_src[:, VECTOR_M:P, :, 2:4], ACT.Copy)
+        nc.vector.tensor_copy(w1_dst[:, :, :, 0:2], w1_src[:, :, :, 0:2])
+        nc.vector.tensor_copy(w1_dst[:, 0:VECTOR_M, :, 2:4], w1_src[:, 0:VECTOR_M, :, 2:4])
+        for c0 in range(0, H, 256):
+            nc.vector.quantize_mx(
+                out=w1_code[:, c0 : c0 + 256].bitcast(FP8X4),
+                scales=w1_scale[:, c0 : c0 + 256],
+                in_=w1_flat[:, c0 * PACK : (c0 + 256) * PACK],
+            )
         gather_words(j0, GATHERS[-1], "w1_bf")
 
         w2_bf = keep.tile([P, N * PACK], BF16, name="w2_bf", align_bytes=64)
         nc.scalar.activation(
             w2_bf[:].rearrange("p (c i j) -> p c j i", i=2, j=PACK),
-            w2_raw.rearrange("p j (c i) -> p c j i", i=2),
+            w2_raw[:].rearrange("p j (c i) -> p c j i", i=2),
             ACT.Copy,
         )
         w2_code = keep.tile([P, N], U32, name="w2_code", align_bytes=64)
@@ -200,13 +178,14 @@ def tile_picked_ypart_gauss_p_kernel(tc, x_words, x_scales, w1, w2, noise, obs, 
             )
             accs[g] = acc
 
+        def square(g):
+            j0, j1 = GROUPS[g]
+            nc.scalar.activation(sq[:, j0:j1], accs[g][:, 0 : j1 - j0], ACT.Square, bias=obs_col)
+
         def likelihood(g):
             j0, j1 = GROUPS[g]
-            cols = slice(j0, j1)
-            squares = sq[:, cols]
-            nc.scalar.activation(squares, accs[g][:, 0 : j1 - j0], ACT.Square, bias=obs_col)
-            nc.scalar.activation(res[:, cols], squares, ACT.Exp, scale=-0.5)
-            nc.sync.dma_start(out[:, cols], res[:, cols])
+            nc.scalar.activation(res[:, j0:j1], sq[:, j0:j1], ACT.Exp, scale=-0.5)
+            nc.sync.dma_start(out[:, j0:j1], res[:, j0:j1])
 
         add_noise(0)
         rectify(0)
@@ -219,11 +198,13 @@ def tile_picked_ypart_gauss_p_kernel(tc, x_words, x_scales, w1, w2, noise, obs, 
         second_layer(0)
         add_noise(4)
         rectify(4)
+        square(0)
         likelihood(0)
         add_noise(5)
         rectify(5)
         second_layer(1)
         add_noise(6)
+        square(1)
         likelihood(1)
         second_layer(2)
         rectify(6)
@@ -231,6 +212,9 @@ def tile_picked_ypart_gauss_p_kernel(tc, x_words, x_scales, w1, w2, noise, obs, 
         rectify(7)
         second_layer(3)
         second_layer(4)
+        square(2)
+        square(3)
         likelihood(2)
+        square(4)
         likelihood(3)
         likelihood(4)

@@ -20,10 +20,11 @@ PACK = 4
 CHUNK = 128
 VECTOR_M = 44
 SCALE_ROW = 112
-NOISE_PIECES = (256,) * 4
+NOISE_PIECES = (256, 256, 256, 128, 128)
 GATHERS = (768, 256)
-ADDS = tuple((c * CHUNK, (c + 1) * CHUNK) for c in range(8))
-GROUPS = ((0, 256), (256, 512), (512, 768), (768, 896), (896, 1024))
+ADDS = tuple((c * CHUNK, (c + 1) * CHUNK) for c in range(7)) + ((896, 960), (960, 1024))
+GROUPS = ((0, 256), (256, 512), (512, 640), (640, 768), (768, 896), (896, 960), (960, 1024))
+STORES = {256: 0, 512: 256, 768: 512, 896: 768, 1024: 896}
 VECTOR_RELU_FROM = 768
 
 
@@ -31,8 +32,8 @@ def tile_picked_ypart_gauss_p_kernel(tc, x_words, x_scales, w1, w2, noise, obs, 
     nc = tc.nc
     with ExitStack() as ctx:
         keep = ctx.enter_context(tc.tile_pool(name="keep", bufs=1))
-        psum1 = ctx.enter_context(tc.psum_pool(name="psum1", bufs=5))
-        psum2 = ctx.enter_context(tc.psum_pool(name="psum2", bufs=3))
+        psum1 = ctx.enter_context(tc.psum_pool(name="psum1", bufs=4))
+        psum2 = ctx.enter_context(tc.psum_pool(name="psum2", bufs=4))
 
         offsets = keep.tile([P, S // 16], U16, name="offsets")
         table_scales = keep.tile([P, T], U8, name="table_scales", tag="table_scales", align_bytes=64)
@@ -185,7 +186,8 @@ def tile_picked_ypart_gauss_p_kernel(tc, x_words, x_scales, w1, w2, noise, obs, 
         def likelihood(g):
             j0, j1 = GROUPS[g]
             nc.scalar.activation(res[:, j0:j1], sq[:, j0:j1], ACT.Exp, scale=-0.5)
-            nc.sync.dma_start(out[:, j0:j1], res[:, j0:j1])
+            if j1 in STORES:
+                nc.sync.dma_start(out[:, STORES[j1] : j1], res[:, STORES[j1] : j1])
 
         add_noise(0)
         rectify(0)
@@ -204,17 +206,25 @@ def tile_picked_ypart_gauss_p_kernel(tc, x_words, x_scales, w1, w2, noise, obs, 
         rectify(5)
         second_layer(1)
         add_noise(6)
+        second_layer(2)
         square(1)
         likelihood(1)
-        second_layer(2)
-        rectify(6)
         add_noise(7)
-        rectify(7)
+        add_noise(8)
+        rectify(6)
         second_layer(3)
+        rectify(7)
+        rectify(8)
         second_layer(4)
+        second_layer(5)
+        second_layer(6)
         square(2)
-        square(3)
         likelihood(2)
+        square(3)
         square(4)
         likelihood(3)
+        square(5)
         likelihood(4)
+        square(6)
+        likelihood(5)
+        likelihood(6)

@@ -69,7 +69,7 @@ def tile_picked_ypart_gauss_p_kernel(tc, x_words, x_scales, w1, w2, noise, obs, 
             nz = late[:, PACK * n0 : PACK * (n0 + width)].rearrange("p (t n) -> p t n", t=PACK)
             nc.sync.dma_start(nz, noise_rows[:, :, n0 : n0 + width])
             noise_chunk.extend(nz[:, :, c0 : c0 + CHUNK] for c0 in range(0, width, CHUNK))
-            if piece == 0:
+            if piece == 2:
                 nc.sync.dma_start(obs_col, obs)
             n0 = n0 + width
 
@@ -95,11 +95,11 @@ def tile_picked_ypart_gauss_p_kernel(tc, x_words, x_scales, w1, w2, noise, obs, 
         nc.scalar.activation(w1_dst[:, VECTOR_M:P, :, 2:4], w1_src[:, VECTOR_M:P, :, 2:4], ACT.Copy)
         nc.vector.tensor_copy(w1_dst[:, :, :, 0:2], w1_src[:, :, :, 0:2])
         nc.vector.tensor_copy(w1_dst[:, 0:VECTOR_M, :, 2:4], w1_src[:, 0:VECTOR_M, :, 2:4])
-        for c0 in range(0, H, 256):
+        for c0, c1 in ((0, 256), (256, 384), (384, 512)):
             nc.vector.quantize_mx(
-                out=w1_code[:, c0 : c0 + 256].bitcast(FP8X4),
-                scales=w1_scale[:, c0 : c0 + 256],
-                in_=w1_flat[:, c0 * PACK : (c0 + 256) * PACK],
+                out=w1_code[:, c0:c1].bitcast(FP8X4),
+                scales=w1_scale[:, c0:c1],
+                in_=w1_flat[:, c0 * PACK : c1 * PACK],
             )
         gather_words(j0, GATHERS[-1], "w1_bf")
 
@@ -125,7 +125,7 @@ def tile_picked_ypart_gauss_p_kernel(tc, x_words, x_scales, w1, w2, noise, obs, 
 
         def first_layer(c):
             bank = psum1.tile([P, PACK, CHUNK], F32, name="bank")
-            for t in range(PACK):
+            for t in range(PACK) if c == 0 else reversed(range(PACK)):
                 tcols = slice(t * P, (t + 1) * P)
                 nc.tensor.matmul_mx(
                     out=bank[:, t, :],

@@ -21,7 +21,7 @@ CHUNK = 128
 VECTOR_M = 44
 SCALE_ROW = 112
 NOISE_PIECES = (256, 256, 256, 128, 128)
-GATHERS = (768, 256)
+GATHERS = (896, 128)
 ADDS = tuple((c * CHUNK, (c + 1) * CHUNK) for c in range(7)) + ((896, 960), (960, 1024))
 GROUPS = ((0, 256), (256, 512), (512, 640), (640, 768), (768, 896), (896, 960), (960, 1024))
 STORES = {256: 0, 512: 256, 768: 512, 896: 768, 1024: 896}
@@ -69,7 +69,7 @@ def tile_picked_ypart_gauss_p_kernel(tc, x_words, x_scales, w1, w2, noise, obs, 
             nz = late[:, PACK * n0 : PACK * (n0 + width)].rearrange("p (t n) -> p t n", t=PACK)
             nc.sync.dma_start(nz, noise_rows[:, :, n0 : n0 + width])
             noise_chunk.extend(nz[:, :, c0 : c0 + CHUNK] for c0 in range(0, width, CHUNK))
-            if piece == 2:
+            if piece == 0:
                 nc.sync.dma_start(obs_col, obs)
             n0 = n0 + width
 

@@ -69,7 +69,7 @@ def tile_picked_ypart_gauss_p_kernel(tc, x_words, x_scales, w1, w2, noise, obs, 
             nz = late[:, PACK * n0 : PACK * (n0 + width)].rearrange("p (t n) -> p t n", t=PACK)
             nc.sync.dma_start(nz, noise_rows[:, :, n0 : n0 + width])
             noise_chunk.extend(nz[:, :, c0 : c0 + CHUNK] for c0 in range(0, width, CHUNK))
-            if piece == 0:
+            if piece == 2:
                 nc.sync.dma_start(obs_col, obs)
             n0 = n0 + width
 
@@ -95,7 +95,7 @@ def tile_picked_ypart_gauss_p_kernel(tc, x_words, x_scales, w1, w2, noise, obs, 
         nc.scalar.activation(w1_dst[:, VECTOR_M:P, :, 2:4], w1_src[:, VECTOR_M:P, :, 2:4], ACT.Copy)
         nc.vector.tensor_copy(w1_dst[:, :, :, 0:2], w1_src[:, :, :, 0:2])
         nc.vector.tensor_copy(w1_dst[:, 0:VECTOR_M, :, 2:4], w1_src[:, 0:VECTOR_M, :, 2:4])
-        for c0, c1 in ((0, 256), (256, 384), (384, 512)):
+        for c0, c1 in ((0, 128), (128, 256), (256, 384), (384, 512)):
             nc.vector.quantize_mx(
                 out=w1_code[:, c0:c1].bitcast(FP8X4),
                 scales=w1_scale[:, c0:c1],

@@ -18,13 +18,15 @@ ALU = mybir.AluOpType
 P = 128
 PACK = 4
 CHUNK = 128
-VECTOR_M = 44
 SCALE_ROW = 112
 NOISE_PIECES = (256, 256, 256, 128, 128)
-GATHERS = (896, 128)
+GATHERS = (256, 256, 256)
+LAST_GATHER = 256
+HELD = (3,)
+PIECE_BYTES = 256 * PACK * 4
 ADDS = tuple((c * CHUNK, (c + 1) * CHUNK) for c in range(7)) + ((896, 960), (960, 1024))
-GROUPS = ((0, 256), (256, 512), (512, 640), (640, 768), (768, 896), (896, 960), (960, 1024))
-STORES = {256: 0, 512: 256, 768: 512, 896: 768, 1024: 896}
+GROUPS = ((128, 384), (0, 128), (384, 640), (640, 768), (768, 896), (896, 960), (960, 1024))
+STORES = {1: (0, 384), 3: (384, 768), 4: (768, 896), 6: (896, 1024)}
 VECTOR_RELU_FROM = 768
 
 
@@ -32,25 +34,26 @@ def tile_picked_ypart_gauss_p_kernel(tc, x_words, x_scales, w1, w2, noise, obs, 
     nc = tc.nc
     with ExitStack() as ctx:
         keep = ctx.enter_context(tc.tile_pool(name="keep", bufs=1))
+        staged = ctx.enter_context(tc.tile_pool(name="staged", bufs=1))
         psum1 = ctx.enter_context(tc.psum_pool(name="psum1", bufs=4))
         psum2 = ctx.enter_context(tc.psum_pool(name="psum2", bufs=4))
 
         offsets = keep.tile([P, S // 16], U16, name="offsets")
-        table_scales = keep.tile([P, T], U8, name="table_scales", tag="table_scales", align_bytes=64)
-        table_words = keep.tile([P, T], U32, name="table_words", align_bytes=64)
+        table_scales = staged.tile([P, T], U8, name="table_scales", offset=PIECE_BYTES - T // 2, align_bytes=64)
+        table_words = keep.tile([P, T], U32, name="table_words", tag="table_words", align_bytes=64)
 
-        picked_scales = keep.tile([P, S], U8, name="picked_scales", align_bytes=64)
+        picked_scales = staged.tile([P, S], U8, name="picked_scales", offset=3 * PIECE_BYTES - S // 2, align_bytes=64)
         x_scale = keep.tile([P, S], U8, name="x_scale", align_bytes=64)
 
         nc.sync.dma_start(offsets[:], offs)
         nc.scalar.dma_start(table_scales[SCALE_ROW:P, :].bitcast(I32), x_scales[0].bitcast(I32))
+        w1_raw = keep.tile([P, PACK, H], F32, name="w1_raw", align_bytes=64)
+        nc.sync.dma_start(w1_raw[:], w1.rearrange("(p j) c -> p j c", j=PACK))
         nc.sync.dma_start(table_words[:].bitcast(I32), x_words[0].rearrange("p n r -> p (n r)").bitcast(I32))
         nc.vector.memset(table_scales[0:SCALE_ROW, :].bitcast(I32), 0)
         nc.vector.memset(x_scale[:].bitcast(I32), 0)
 
-        w1_raw = keep.tile([P, PACK, H], F32, name="w1_raw", align_bytes=64)
-        nc.sync.dma_start(w1_raw[:], w1.rearrange("(p j) c -> p j c", j=PACK))
-        w2_raw = keep.tile([P, PACK, N], F32, name="w2_raw", align_bytes=64)
+        w2_raw = keep.tile([P, PACK, N], F32, name="w2_raw", tag="w2_raw", align_bytes=64)
         nc.sync.dma_start(w2_raw[:], w2.rearrange("(p j) n -> p j n", j=PACK))
         noise_rows = noise.rearrange("(p t) n -> p t n", t=PACK)
 
@@ -61,29 +64,21 @@ def tile_picked_ypart_gauss_p_kernel(tc, x_words, x_scales, w1, w2, noise, obs, 
                 picked_scales[SCALE_ROW + 4 * q : SCALE_ROW + 4 * q + 4, :].bitcast(I32),
             )
 
-        late = keep.tile([P, PACK * S + 8], F32, name="late", tag="table_scales", align_bytes=64)
-        obs_col = late[:, PACK * S : PACK * S + 1]
+        early = [
+            staged.tile([P, PACK * 256], F32, name="early%d" % i, offset=i * PIECE_BYTES, align_bytes=64) for i in range(3)
+        ]
+        late = staged.tile([P, PACK * 256 + 8], F32, name="late", offset=3 * PIECE_BYTES, align_bytes=64)
+        obs_col = late[:, PACK * 256 : PACK * 256 + 1]
         noise_chunk = []
         n0 = 0
         for piece, width in enumerate(NOISE_PIECES):
-            nz = late[:, PACK * n0 : PACK * (n0 + width)].rearrange("p (t n) -> p t n", t=PACK)
+            room = early[piece][:] if piece < 3 else late[:, PACK * (n0 - 768) : PACK * (n0 - 768 + width)]
+            nz = room.rearrange("p (t n) -> p t n", t=PACK)
             nc.sync.dma_start(nz, noise_rows[:, :, n0 : n0 + width])
             noise_chunk.extend(nz[:, :, c0 : c0 + CHUNK] for c0 in range(0, width, CHUNK))
             if piece == 2:
                 nc.sync.dma_start(obs_col, obs)
             n0 = n0 + width
-
-        x_code = []
-
-        def gather_words(j0, width, tag):
-            codes = keep.tile([P, width], U32, name="x_code%d" % j0, tag=tag, align_bytes=64)
-            nc.vector.tensor_copy(codes[:], table_words[:].indirect(offsets[:, j0 // 16 : (j0 + width) // 16]))
-            x_code.extend(codes[:, c0 : c0 + CHUNK] for c0 in range(0, width, CHUNK))
-
-        j0 = 0
-        for width in GATHERS[:-1]:
-            gather_words(j0, width, "x_code%d" % j0)
-            j0 = j0 + width
 
         w1_bf = keep.tile([P, PACK, P, PACK], BF16, name="w1_bf", tag="w1_bf", align_bytes=64)
         w1_dst = w1_bf[:].rearrange("p t m j -> p m j t")
@@ -92,16 +87,21 @@ def tile_picked_ypart_gauss_p_kernel(tc, x_words, x_scales, w1, w2, noise, obs, 
         w1_scale = keep.tile([P, H], U8, name="w1_scale", align_bytes=64)
         w1_flat = w1_bf[:].rearrange("p t m j -> p (t m j)")
 
-        nc.scalar.activation(w1_dst[:, VECTOR_M:P, :, 2:4], w1_src[:, VECTOR_M:P, :, 2:4], ACT.Copy)
+        nc.scalar.activation(w1_dst[:, :, :, 2:4], w1_src[:, :, :, 2:4], ACT.Copy)
         nc.vector.tensor_copy(w1_dst[:, :, :, 0:2], w1_src[:, :, :, 0:2])
-        nc.vector.tensor_copy(w1_dst[:, 0:VECTOR_M, :, 2:4], w1_src[:, 0:VECTOR_M, :, 2:4])
-        for c0, c1 in ((0, 128), (128, 256), (256, 384), (384, 512)):
+        for c0, c1 in ((0, 256), (256, 512)):
             nc.vector.quantize_mx(
                 out=w1_code[:, c0:c1].bitcast(FP8X4),
                 scales=w1_scale[:, c0:c1],
                 in_=w1_flat[:, c0 * PACK : c1 * PACK],
             )
-        gather_words(j0, GATHERS[-1], "w1_bf")
+        x_code = keep.tile([P, S - LAST_GATHER], U32, name="x_code", tag="w1_bf", align_bytes=64)
+        j0 = 0
+        for width in GATHERS:
+            nc.vector.tensor_copy(
+                x_code[:, j0 : j0 + width], table_words[:].indirect(offsets[:, j0 // 16 : (j0 + width) // 16])
+            )
+            j0 = j0 + width
 
         w2_bf = keep.tile([P, N * PACK], BF16, name="w2_bf", align_bytes=64)
         nc.scalar.activation(
@@ -112,26 +112,38 @@ def tile_picked_ypart_gauss_p_kernel(tc, x_words, x_scales, w1, w2, noise, obs, 
         w2_code = keep.tile([P, N], U32, name="w2_code", align_bytes=64)
         w2_scale = keep.tile([P, N], U8, name="w2_scale", align_bytes=64)
         nc.vector.quantize_mx(out=w2_code[:].bitcast(FP8X4), scales=w2_scale[:], in_=w2_bf[:])
+        x_last = keep.tile([P, LAST_GATHER], U32, name="x_last", tag="w2_raw", align_bytes=64)
+        nc.vector.tensor_copy(x_last[:], table_words[:].indirect(offsets[:, (S - LAST_GATHER) // 16 : S // 16]))
 
+        held = {c: keep.tile([P, CHUNK * PACK], BF16, name="pre%d" % c, tag="pre%d" % c, align_bytes=64) for c in HELD}
         pre = keep.tile([P, S * PACK], BF16, name="pre", align_bytes=64)
+        codes = [x_code[:, c0 : c0 + CHUNK] for c0 in range(0, S - LAST_GATHER, CHUNK)]
+        codes.extend(x_last[:, c0 : c0 + CHUNK] for c0 in range(0, LAST_GATHER, CHUNK))
+
+        def summed(j0, j1):
+            if j0 // CHUNK in held:
+                return held[j0 // CHUNK][:]
+            return pre[:, j0 * PACK : j1 * PACK]
+
         hid = keep.tile([P, S * PACK], BF16, name="hid", align_bytes=64)
         h_code = keep.tile([P, S], U32, name="h_code", align_bytes=64)
         h_scale = keep.tile([P, S], U8, name="h_scale", align_bytes=64)
         sq = keep.tile([P, S], F32, name="sq", align_bytes=64)
         res = keep.tile([P, S], F32, name="res", align_bytes=64)
 
+        woven = []
         banks = {}
         accs = {}
 
         def first_layer(c):
             bank = psum1.tile([P, PACK, CHUNK], F32, name="bank")
-            for t in range(PACK) if c == 0 else reversed(range(PACK)):
+            for t in range(PACK):
                 tcols = slice(t * P, (t + 1) * P)
                 nc.tensor.matmul_mx(
                     out=bank[:, t, :],
                     lhsT=w1_code[:, tcols].bitcast(FP8X4),
                     lhsT_scale=w1_scale[:, tcols],
-                    rhs=x_code[c].bitcast(FP8X4),
+                    rhs=codes[c].bitcast(FP8X4),
                     rhs_scale=x_scale[:, c * CHUNK : (c + 1) * CHUNK],
                     start=True,
                     stop=True,
@@ -145,34 +157,55 @@ def tile_picked_ypart_gauss_p_kernel(tc, x_words, x_scales, w1, w2, noise, obs, 
                 first_layer(c)
             inner = slice(j0 - c * CHUNK, j1 - c * CHUNK)
             nc.vector.tensor_tensor(
-                pre[:, j0 * PACK : j1 * PACK].rearrange("p (c i t) -> p c t i", i=2, t=PACK),
+                summed(j0, j1).rearrange("p (c i t) -> p c t i", i=2, t=PACK),
                 banks[c][:, :, inner].rearrange("p t (c i) -> p c t i", i=2),
                 noise_chunk[c][:, :, inner].rearrange("p t (c i) -> p c t i", i=2),
                 ALU.add,
+            )
+
+        def add_noise_on_gpsimd(c):
+            first_layer(c)
+            product = keep.tile([P, PACK, CHUNK], F32, name="product", align_bytes=64)
+            planes = keep.tile([P, PACK, CHUNK], BF16, name="planes", tag="table_words", align_bytes=64)
+            nc.scalar.copy(product[:], banks[c][:])
+            nc.gpsimd.tensor_tensor(planes[:], product[:], noise_chunk[c], ALU.add)
+            return planes
+
+        def rectify_planes(planes):
+            hid_first = keep.tile([P, CHUNK * PACK], BF16, name="hid_first", tag="pre3", align_bytes=64)
+            woven.append(hid_first)
+            nc.scalar.activation(
+                hid_first[:].rearrange("p (c i t) -> p c t i", i=4, t=PACK),
+                planes[:].rearrange("p t (c i) -> p c t i", i=4),
+                ACT.Relu,
             )
 
         def rectify(a):
             j0, j1 = ADDS[a]
             span = slice(j0 * PACK, j1 * PACK)
             if j0 >= VECTOR_RELU_FROM:
-                nc.vector.tensor_scalar_max(hid[:, span], pre[:, span], 0.0)
+                nc.vector.tensor_scalar_max(hid[:, span], summed(j0, j1), 0.0)
             else:
-                nc.scalar.activation(hid[:, span], pre[:, span], ACT.Relu)
+                nc.scalar.activation(hid[:, span], summed(j0, j1), ACT.Relu)
 
         def second_layer(g):
             j0, j1 = GROUPS[g]
             cols = slice(j0, j1)
+            group_code = h_code[:, cols]
+            if j0 == 0:
+                first_code = staged.tile([P, CHUNK], U32, name="first_code", offset=2 * PIECE_BYTES, align_bytes=64)
+                group_code = first_code[:]
             nc.vector.quantize_mx(
-                out=h_code[:, cols].bitcast(FP8X4),
+                out=group_code.bitcast(FP8X4),
                 scales=h_scale[:, cols],
-                in_=hid[:, j0 * PACK : j1 * PACK],
+                in_=woven[0][:] if j0 == 0 else hid[:, j0 * PACK : j1 * PACK],
             )
             acc = psum2.tile([P, 256], F32, name="acc")
             nc.tensor.matmul_mx(
                 out=acc[:, 0 : j1 - j0],
                 lhsT=w2_code[:].bitcast(FP8X4),
                 lhsT_scale=w2_scale[:],
-                rhs=h_code[:, cols].bitcast(FP8X4),
+                rhs=group_code.bitcast(FP8X4),
                 rhs_scale=h_scale[:, cols],
                 start=True,
                 stop=True,
@@ -186,17 +219,18 @@ def tile_picked_ypart_gauss_p_kernel(tc, x_words, x_scales, w1, w2, noise, obs, 
         def likelihood(g):
             j0, j1 = GROUPS[g]
             nc.scalar.activation(res[:, j0:j1], sq[:, j0:j1], ACT.Exp, scale=-0.5)
-            if j1 in STORES:
-                nc.sync.dma_start(out[:, STORES[j1] : j1], res[:, STORES[j1] : j1])
+            if g in STORES:
+                s0, s1 = STORES[g]
+                nc.sync.dma_start(out[:, s0:s1], res[:, s0:s1])
 
-        add_noise(0)
-        rectify(0)
+        planes = add_noise_on_gpsimd(0)
         add_noise(1)
         rectify(1)
         add_noise(2)
         rectify(2)
         add_noise(3)
         rectify(3)
+        rectify_planes(planes)
         second_layer(0)
         add_noise(4)
         rectify(4)

@@ -40,7 +40,7 @@ def tile_picked_ypart_gauss_p_kernel(tc, x_words, x_scales, w1, w2, noise, obs, 
 
         offsets = keep.tile([P, S // 16], U16, name="offsets")
         table_scales = staged.tile([P, T], U8, name="table_scales", offset=PIECE_BYTES - T // 2, align_bytes=64)
-        table_words = keep.tile([P, T], U32, name="table_words", tag="table_words", align_bytes=64)
+        table_words = keep.tile([P, T], U32, name="table_words", align_bytes=64)
 
         picked_scales = staged.tile([P, S], U8, name="picked_scales", offset=3 * PIECE_BYTES - S // 2, align_bytes=64)
         x_scale = keep.tile([P, S], U8, name="x_scale", align_bytes=64)
@@ -166,7 +166,7 @@ def tile_picked_ypart_gauss_p_kernel(tc, x_words, x_scales, w1, w2, noise, obs, 
         def add_noise_on_gpsimd(c):
             first_layer(c)
             product = keep.tile([P, PACK, CHUNK], F32, name="product", align_bytes=64)
-            planes = keep.tile([P, PACK, CHUNK], BF16, name="planes", tag="table_words", align_bytes=64)
+            planes = keep.tile([P, PACK, CHUNK], BF16, name="planes", align_bytes=64)
             nc.scalar.copy(product[:], banks[c][:])
             nc.gpsimd.tensor_tensor(planes[:], product[:], noise_chunk[c], ALU.add)
             return planes

from contextlib import ExitStack

import concourse.mybir as mybir

K, T, S, H, N = 512, 2048, 1024, 512, 128
FLOPS = 2 * K * H * S + 2 * H * N * S

F32 = mybir.dt.float32
BF16 = mybir.dt.bfloat16
I32 = mybir.dt.int32
U32 = mybir.dt.uint32
U16 = mybir.dt.uint16
U8 = mybir.dt.uint8
FP8X4 = mybir.dt.float8_e4m3fn_x4
ACT = mybir.ActivationFunctionType
ALU = mybir.AluOpType

P = 128
PACK = 4
CHUNK = 128
SCALE_ROW = 112
NOISE_PIECES = (256, 256, 256, 128, 128)
GATHERS = (256, 256, 256)
LAST_GATHER = 256
HELD = (3,)
PIECE_BYTES = 256 * PACK * 4
ADDS = tuple((c * CHUNK, (c + 1) * CHUNK) for c in range(7)) + ((896, 960), (960, 1024))
GROUPS = ((128, 384), (0, 128), (384, 640), (640, 768), (768, 896), (896, 960), (960, 1024))
STORES = {1: (0, 384), 3: (384, 768), 4: (768, 896), 6: (896, 1024)}
VECTOR_RELU_FROM = 768


def tile_picked_ypart_gauss_p_kernel(tc, x_words, x_scales, w1, w2, noise, obs, offs, out):
    nc = tc.nc
    with ExitStack() as ctx:
        keep = ctx.enter_context(tc.tile_pool(name="keep", bufs=1))
        staged = ctx.enter_context(tc.tile_pool(name="staged", bufs=1))
        psum1 = ctx.enter_context(tc.psum_pool(name="psum1", bufs=4))
        psum2 = ctx.enter_context(tc.psum_pool(name="psum2", bufs=4))

        offsets = keep.tile([P, S // 16], U16, name="offsets")
        table_scales = staged.tile([P, T], U8, name="table_scales", offset=PIECE_BYTES - T // 2, align_bytes=64)
        table_words = keep.tile([P, T], U32, name="table_words", align_bytes=64)

        picked_scales = staged.tile([P, S], U8, name="picked_scales", offset=3 * PIECE_BYTES - S // 2, align_bytes=64)
        x_scale = keep.tile([P, S], U8, name="x_scale", align_bytes=64)

        nc.sync.dma_start(offsets[:], offs)
        nc.scalar.dma_start(table_scales[SCALE_ROW:P, :].bitcast(I32), x_scales[0].bitcast(I32))
        w1_raw = keep.tile([P, PACK, H], F32, name="w1_raw", align_bytes=64)
        nc.sync.dma_start(w1_raw[:], w1.rearrange("(p j) c -> p j c", j=PACK))
        nc.sync.dma_start(table_words[:].bitcast(I32), x_words[0].rearrange("p n r -> p (n r)").bitcast(I32))
        nc.vector.memset(table_scales[0:SCALE_ROW, :].bitcast(I32), 0)
        nc.vector.memset(x_scale[:].bitcast(I32), 0)

        w2_raw = keep.tile([P, PACK, N], F32, name="w2_raw", tag="w2_raw", align_bytes=64)
        nc.sync.dma_start(w2_raw[:], w2.rearrange("(p j) n -> p j n", j=PACK))
        noise_rows = noise.rearrange("(p t) n -> p t n", t=PACK)

        nc.vector.tensor_copy(picked_scales[:], table_scales[:].indirect(offsets[:]))
        for q in range(4):
            nc.sync.dma_start(
                x_scale[32 * q : 32 * q + 4, :].bitcast(I32),
                picked_scales[SCALE_ROW + 4 * q : SCALE_ROW + 4 * q + 4, :].bitcast(I32),
            )

        early = [
            staged.tile([P, PACK * 256], F32, name="early%d" % i, offset=i * PIECE_BYTES, align_bytes=64) for i in range(3)
        ]
        late = staged.tile([P, PACK * 256 + 8], F32, name="late", offset=3 * PIECE_BYTES, align_bytes=64)
        obs_col = late[:, PACK * 256 : PACK * 256 + 1]
        noise_chunk = []
        n0 = 0
        for piece, width in enumerate(NOISE_PIECES):
            room = early[piece][:] if piece < 3 else late[:, PACK * (n0 - 768) : PACK * (n0 - 768 + width)]
            nz = room.rearrange("p (t n) -> p t n", t=PACK)
            nc.sync.dma_start(nz, noise_rows[:, :, n0 : n0 + width])
            noise_chunk.extend(nz[:, :, c0 : c0 + CHUNK] for c0 in range(0, width, CHUNK))
            if piece == 2:
                nc.sync.dma_start(obs_col, obs)
            n0 = n0 + width

        w1_bf = keep.tile([P, PACK, P, PACK], BF16, name="w1_bf", tag="w1_bf", align_bytes=64)
        w1_dst = w1_bf[:].rearrange("p t m j -> p m j t")
        w1_src = w1_raw[:].rearrange("p j (m t) -> p m j t", t=PACK)
        w1_code = keep.tile([P, H], U32, name="w1_code", align_bytes=64)
        w1_scale = keep.tile([P, H], U8, name="w1_scale", align_bytes=64)
        w1_flat = w1_bf[:].rearrange("p t m j -> p (t m j)")

        nc.scalar.activation(w1_dst[:, :, :, 2:4], w1_src[:, :, :, 2:4], ACT.Copy)
        nc.vector.tensor_copy(w1_dst[:, :, :, 0:2], w1_src[:, :, :, 0:2])
        for c0, c1 in ((0, 256), (256, 512)):
            nc.vector.quantize_mx(
                out=w1_code[:, c0:c1].bitcast(FP8X4),
                scales=w1_scale[:, c0:c1],
                in_=w1_flat[:, c0 * PACK : c1 * PACK],
            )
        x_code = keep.tile([P, S - LAST_GATHER], U32, name="x_code", tag="w1_bf", align_bytes=64)
        j0 = 0
        for width in GATHERS:
            nc.vector.tensor_copy(
                x_code[:, j0 : j0 + width], table_words[:].indirect(offsets[:, j0 // 16 : (j0 + width) // 16])
            )
            j0 = j0 + width

        w2_bf = keep.tile([P, N * PACK], BF16, name="w2_bf", align_bytes=64)
        nc.scalar.activation(
            w2_bf[:].rearrange("p (c i j) -> p c j i", i=2, j=PACK),
            w2_raw[:].rearrange("p j (c i) -> p c j i", i=2),
            ACT.Copy,
        )
        w2_code = keep.tile([P, N], U32, name="w2_code", align_bytes=64)
        w2_scale = keep.tile([P, N], U8, name="w2_scale", align_bytes=64)
        nc.vector.quantize_mx(out=w2_code[:].bitcast(FP8X4), scales=w2_scale[:], in_=w2_bf[:])
        x_last = keep.tile([P, LAST_GATHER], U32, name="x_last", tag="w2_raw", align_bytes=64)
        nc.vector.tensor_copy(x_last[:], table_words[:].indirect(offsets[:, (S - LAST_GATHER) // 16 : S // 16]))

        held = {c: keep.tile([P, CHUNK * PACK], BF16, name="pre%d" % c, tag="pre%d" % c, align_bytes=64) for c in HELD}
        pre = keep.tile([P, S * PACK], BF16, name="pre", align_bytes=64)
        codes = [x_code[:, c0 : c0 + CHUNK] for c0 in range(0, S - LAST_GATHER, CHUNK)]
        codes.extend(x_last[:, c0 : c0 + CHUNK] for c0 in range(0, LAST_GATHER, CHUNK))

        def summed(j0, j1):
            if j0 // CHUNK in held:
                return held[j0 // CHUNK][:]
            return pre[:, j0 * PACK : j1 * PACK]

        hid = keep.tile([P, S * PACK], BF16, name="hid", align_bytes=64)
        h_code = keep.tile([P, S], U32, name="h_code", align_bytes=64)
        h_scale = keep.tile([P, S], U8, name="h_scale", align_bytes=64)
        sq = keep.tile([P, S], F32, name="sq", align_bytes=64)
        res = keep.tile([P, S], F32, name="res", align_bytes=64)

        woven = []
        banks = {}
        accs = {}

        def first_layer(c):
            bank = psum1.tile([P, PACK, CHUNK], F32, name="bank")
            for t in range(PACK):
                tcols = slice(t * P, (t + 1) * P)
                nc.tensor.matmul_mx(
                    out=bank[:, t, :],
                    lhsT=w1_code[:, tcols].bitcast(FP8X4),
                    lhsT_scale=w1_scale[:, tcols],
                    rhs=codes[c].bitcast(FP8X4),
                    rhs_scale=x_scale[:, c * CHUNK : (c + 1) * CHUNK],
                    start=True,
                    stop=True,
                )
            banks[c] = bank

        def add_noise(a):
            j0, j1 = ADDS[a]
            c = j0 // CHUNK
            if j0 % CHUNK == 0:
                first_layer(c)
            inner = slice(j0 - c * CHUNK, j1 - c * CHUNK)
            nc.vector.tensor_tensor(
                summed(j0, j1).rearrange("p (c i t) -> p c t i", i=2, t=PACK),
                banks[c][:, :, inner].rearrange("p t (c i) -> p c t i", i=2),
                noise_chunk[c][:, :, inner].rearrange("p t (c i) -> p c t i", i=2),
                ALU.add,
            )

        def add_noise_on_gpsimd(c):
            first_layer(c)
            product = keep.tile([P, PACK, CHUNK], F32, name="product", align_bytes=64)
            planes = keep.tile([P, PACK, CHUNK], BF16, name="planes", align_bytes=64)
            nc.scalar.copy(product[:], banks[c][:])
            nc.gpsimd.tensor_tensor(planes[:], product[:], noise_chunk[c], ALU.add)
            return planes

        def rectify_planes(planes):
            hid_first = keep.tile([P, CHUNK * PACK], BF16, name="hid_first", tag="pre3", align_bytes=64)
            woven.append(hid_first)
            nc.scalar.activation(
                hid_first[:].rearrange("p (c i t) -> p c t i", i=4, t=PACK),
                planes[:].rearrange("p t (c i) -> p c t i", i=4),
                ACT.Relu,
            )

        def rectify(a):
            j0, j1 = ADDS[a]
            span = slice(j0 * PACK, j1 * PACK)
            if j0 >= VECTOR_RELU_FROM:
                nc.vector.tensor_scalar_max(hid[:, span], summed(j0, j1), 0.0)
            else:
                nc.scalar.activation(hid[:, span], summed(j0, j1), ACT.Relu)

        def second_layer(g):
            j0, j1 = GROUPS[g]
            cols = slice(j0, j1)
            group_code = h_code[:, cols]
            if j0 == 0:
                first_code = staged.tile([P, CHUNK], U32, name="first_code", offset=2 * PIECE_BYTES, align_bytes=64)
                group_code = first_code[:]
            nc.vector.quantize_mx(
                out=group_code.bitcast(FP8X4),
                scales=h_scale[:, cols],
                in_=woven[0][:] if j0 == 0 else hid[:, j0 * PACK : j1 * PACK],
            )
            acc = psum2.tile([P, 256], F32, name="acc")
            nc.tensor.matmul_mx(
                out=acc[:, 0 : j1 - j0],
                lhsT=w2_code[:].bitcast(FP8X4),
                lhsT_scale=w2_scale[:],
                rhs=group_code.bitcast(FP8X4),
                rhs_scale=h_scale[:, cols],
                start=True,
                stop=True,
            )
            accs[g] = acc

        def square(g):
            j0, j1 = GROUPS[g]
            nc.scalar.activation(sq[:, j0:j1], accs[g][:, 0 : j1 - j0], ACT.Square, bias=obs_col)

        def likelihood(g):
            j0, j1 = GROUPS[g]
            nc.scalar.activation(res[:, j0:j1], sq[:, j0:j1], ACT.Exp, scale=-0.5)
            if g in STORES:
                s0, s1 = STORES[g]
                nc.sync.dma_start(out[:, s0:s1], res[:, s0:s1])

        planes = add_noise_on_gpsimd(0)
        add_noise(1)
        rectify(1)
        add_noise(2)
        rectify(2)
        add_noise(3)
        rectify(3)
        rectify_planes(planes)
        second_layer(0)
        add_noise(4)
        rectify(4)
        square(0)
        likelihood(0)
        add_noise(5)
        rectify(5)
        second_layer(1)
        add_noise(6)
        second_layer(2)
        square(1)
        likelihood(1)
        add_noise(7)
        add_noise(8)
        rectify(6)
        second_layer(3)
        rectify(7)
        rectify(8)
        second_layer(4)
        second_layer(5)
        second_layer(6)
        square(2)
        likelihood(2)
        square(3)
        square(4)
        likelihood(3)
        square(5)
        likelihood(4)
        square(6)
        likelihood(5)
        likelihood(6)
